import numpy as np, ml_dtypes
CORES = [6,14,22,30,38,134,142,150,158]
N = 9
QP = 32
def setup_inputs(rng):
    m = 150 * rng.standard_normal((1, QP, 1), dtype=np.float32) + 3 * rng.standard_normal((N, QP, 1), dtype=np.float32)
    m = (m + rng.uniform(100, 300, (1, QP, 1)) * (rng.random((1, QP, 1)) < 0.7) * (rng.random((N, QP, 1)) < 0.5)).astype(np.float32)
    l = 20 * (1 + np.abs(rng.standard_normal((N, QP, 1), dtype=np.float32)))
    return {"o": (l * rng.standard_normal((N, QP, 128), dtype=np.float32) / 4).astype(ml_dtypes.bfloat16), "ml": np.concatenate([m, l], axis=2)}
def setup_inputs_big(rng):
    d = setup_inputs(rng)
    for k in ("o",): d[k] = (d[k].astype(np.float32) * 1048576.0).astype(d[k].dtype)
    return d
def setup_inputs_small(rng):
    d = setup_inputs(rng)
    for k in ("o",): d[k] = (d[k].astype(np.float32) * (1 / 1048576.0)).astype(d[k].dtype)
    return d
def setup_inputs_apart(rng):
    d = setup_inputs(rng)
    f = (10.0 ** rng.permutation(np.linspace(-1.5, 1.5, N))).astype(np.float32).reshape(N, 1, 1)
    for k in ("o",): d[k] = (d[k].astype(np.float32) * f).astype(d[k].dtype)
    return d
def reference(o, ml):
    O, ML = o.astype(np.float64), ml.astype(np.float64)
    m, l = ML[:, :, 0:1], ML[:, :, 1:2]
    f = np.exp(m - m.max(axis=0))
    y = ((f * O).sum(axis=0) / (f * l).sum(axis=0)).astype(ml_dtypes.bfloat16)
    return {"y": np.broadcast_to(y, (N,) + y.shape)}

@@ -1,0 +1,139 @@
+from concourse.bass import DstId, RemoteDMATransfer
+from concourse.mybir import AluOpType, AxisListType, ActivationFunctionType
+
+N, Q, D = 9, 32, 128
+NP = 4
+G = 3
+P = G * Q
+
+SCRATCH = {
+    "land_o": ("dram", [N, NP * 128, 8], "bfloat16"),
+    "land_ml": ("dram", [N, 128, 4], "float32"),
+    "zero": ("sbuf", [128, 2 * Q], "float32"),
+    "mT": ("sbuf", [128, 2 * Q], "float32"),
+    "o_sb": ("sbuf", [128, G, D], "bfloat16"),
+    "V": ("sbuf", [128, Q], "float32"),
+    "mask": ("sbuf", [128, Q], "bfloat16"),
+    "E": ("sbuf", [128, 16], "float32"),
+    "negM": ("sbuf", [128, 1], "float32"),
+    "ch": ("sbuf", [128, 24], "float32"),
+    "lA": ("sbuf", [128, 4], "bfloat16"),
+    "W": ("sbuf", [128, G, Q], "bfloat16"),
+    "r": ("sbuf", [128, 1], "float32"),
+    "y_sb": ("sbuf", [128, D], "bfloat16"),
+    "Pm": ("psum", [128, 512], "float32"),
+    "Pl": ("psum", [128, 512], "float32"),
+    "Pd": ("psum", [128, 512], "float32"),
+    "Po0": ("psum", [128, 512], "float32"),
+    "Po1": ("psum", [128, 512], "float32"),
+}
+SEMAPHORES = ["zs", "ld_ml", "ld_o", "sent", "ml_arr", "o_arr", "ml_in", "o_in", "iota", "cst", "pm", "pl", "nm", "xs",
+              "la", "act", "w0", "w1", "w2", "pd", "po0", "po1", "rs", "yd", "stored"]
+
+
+def rank_program(g, core, T, topo):
+    rank = T.rank_of(core)
+    if rank is None:
+        return
+    S = T.sem
+    sy, ac, ve, te = g.sync, g.scalar, g.vector, g.tensor
+    Sq, Cp = ActivationFunctionType.Square, ActivationFunctionType.Copy
+    A = AluOpType
+
+    ve.memset(T.zero[0:7, :], 0.0).then_inc(S.zs, 1)
+    sy.dma_start(T.land_ml[rank, 0:16, :], T.ml[:]).then_inc(S.ld_ml, 16)
+    ac.dma_start(T.land_o[rank], T.o[:]).then_inc(S.ld_o, 16)
+    sy.wait_ge(S.zs, 1)
+    sy.dma_start(T.land_ml[rank, 16:128, :], T.zero[0:7, :]).then_inc(S.ld_ml, 16)
+
+    g.iota(T.V[0:P, :], [[-1, Q]], 0, 1, allow_small_or_imprecise_dtypes=True).then_inc(S.iota, 1)
+    ve.wait_ge(S.iota, 1)
+    ve.tensor_scalar(T.E[0:N, 0:N], T.V[0:N, 0:N], 0.0, None, A.is_equal).then_inc(S.cst, 1)
+    ve.tensor_scalar(T.E[0:N, N:15], T.V[0:N, N:15], float(-N), None, A.is_equal).then_inc(S.cst, 1)
+    for k in range(G):
+        ve.tensor_scalar(T.mask[Q * k:Q * k + Q, :], T.V[Q * k:Q * k + Q, :], float(Q * k), None,
+                         A.is_equal).then_inc(S.cst, 1)
+
+    others = [T.cores[(rank + k) % N] for k in range(1, N)]
+    usable = 0xFFFF
+    for d in others:
+        assert topo.may_write(core, d)
+        usable &= topo.mask(core, d)
+    eng = [e for e in range(16) if (usable >> e) & 1]
+    ids = []
+    for d in others:
+        rid, pid = topo.addr(d, core)
+        ids.append(DstId(rid=rid, pnc=pid))
+    ml_eng, o_eng = eng[0], [eng[2], eng[4], eng[6], eng[7]]
+    transfers = [RemoteDMATransfer(dst_ids=ids, dma_engine_mask=1 << ml_eng, remote_sem=S.ml_arr,
+                                   srcs=[T.land_ml[rank]], dsts=[T.land_ml[rank] for _ in others])]
+    for p in range(NP):
+        piece = T.land_o[rank, 128 * p:128 * p + 128, :]
+        transfers.append(RemoteDMATransfer(dst_ids=ids, dma_engine_mask=1 << o_eng[p], remote_sem=S.o_arr,
+                                           srcs=[piece], dsts=[piece for _ in others]))
+    g.wait_ge(S.ld_ml, 32)
+    g.wait_ge(S.ld_o, 16)
+    g.remote_dma_fused(transfers, local_sem=S.sent)
+    g.wait_ge(S.sent, 1 + NP)
+
+    sy.wait_ge(S.ld_ml, 32)
+    sy.wait_ge(S.ml_arr, N - 1)
+    sy.dma_start(T.mT[0:N, :], T.land_ml[:, 0:16, :]).then_inc(S.ml_in, 16)
+    for q_, cs in ((sy, (0,)), (ac, (1, 2))):
+        q_.wait_ge(S.ld_o, 16)
+        q_.wait_ge(S.o_arr, (N - 1) * NP)
+        for c in cs:
+            q_.dma_start(T.o_sb[0:P, c, :], T.land_o[c::G]).then_inc(S.o_in, 16)
+
+    te.wait_ge(S.cst, 5)
+    te.wait_ge(S.ml_in, 16)
+    for k in range(G):
+        te.matmul(T.Pm[Q * k:Q * k + Q, 0:N], T.mT[0:N, 0:2 * Q:2], T.E[0:N, G * k:G * k + N], True, True).then_inc(S.pm, 1)
+    for k in range(G):
+        te.matmul(T.Pl[Q * k:Q * k + Q, 0:G], T.mT[0:N, 1:2 * Q:2], T.E[0:N, G * k:G * k + G], True, True).then_inc(S.pl, 1)
+
+    ve.wait_ge(S.pm, G)
+    ve.tensor_reduce(T.negM[0:P, :], T.Pm[0:P, 0:N], AxisListType.X, A.max, negate=True).then_inc(S.nm, 1)
+    ve.wait_ge(S.nm, 1)
+    ve.tensor_scalar(T.ch[0:P, 0:G], T.Pm[0:P, 0:G], T.negM[0:P, 0:1], -16.0, A.add, A.max).then_inc(S.xs, 1)
+    ve.wait_ge(S.pl, G)
+    ve.tensor_copy(T.lA[0:P, 0:G], T.Pl[0:P, 0:G]).then_inc(S.la, 1)
+
+    def col(i):
+        return T.ch[0:P, 4 * i:4 * i + G]
+    ac.wait_ge(S.xs, 1)
+    ac.activation(col(1), col(0), Sq, bias=1.0, scale=1.0 / 16.0).then_inc(S.act, 1)
+    ac.wait_ge(S.act, 1)
+    ac.activation(col(2), col(1), Sq, bias=1.0).then_inc(S.act, 1)
+    for i in (2, 3, 4):
+        ac.wait_ge(S.act, i)
+        ac.activation(col(i + 1), col(i), Sq).then_inc(S.act, 1)
+    f0 = 20
+
+    ac.wait_ge(S.act, 5)
+    ac.wait_ge(S.cst, 5)
+    ac.activation(T.W[0:P, 1, :], T.mask[0:P, :], Cp, scale=T.ch[0:P, f0 + 1:f0 + 2]).then_inc(S.w1, 1)
+    ve.wait_ge(S.act, 5)
+    ve.wait_ge(S.cst, 5)
+    ve.tensor_scalar(T.W[0:P, 0, :], T.mask[0:P, :], T.ch[0:P, f0:f0 + 1], None, A.mult).then_inc(S.w0, 1)
+    ve.tensor_scalar(T.W[0:P, 2, :], T.mask[0:P, :], T.ch[0:P, f0 + 2:f0 + 3], None, A.mult).then_inc(S.w2, 1)
+
+    te.wait_ge(S.la, 1)
+    for c in range(G):
+        te.wait_ge(S["w%d" % c], 1)
+        te.matmul(T.Pd[0:Q, 0:1], T.W[0:P, c, :], T.lA[0:P, c:c + 1], c == 0, c == G - 1).then_inc(S.pd, 1)
+    te.wait_ge(S.o_in, 16 * G)
+    H = D // 2
+    for h, (Po, sem) in enumerate(((T.Po0, S.po0), (T.Po1, S.po1))):
+        for c in range(G):
+            te.matmul(Po[0:Q, 0:H], T.W[0:P, c, :], T.o_sb[0:P, c, H * h:H * h + H], c == 0, c == G - 1).then_inc(sem, 1)
+
+    ve.wait_ge(S.pd, G)
+    ve.reciprocal(T.r[0:Q, :], T.Pd[0:Q, 0:1]).then_inc(S.rs, 1)
+    ve.wait_ge(S.rs, 1)
+    for h, (Po, sem) in enumerate(((T.Po0, S.po0), (T.Po1, S.po1))):
+        ve.wait_ge(sem, G)
+        ve.tensor_scalar(T.y_sb[0:Q, H * h:H * h + H], Po[0:Q, 0:H], T.r[0:Q, 0:1], None, A.mult).then_inc(S.yd, 1)
+    sy.wait_ge(S.yd, 2)
+    sy.dma_start(T.y[:], T.y_sb[0:Q, :]).then_inc(S.stored, 16)
+    sy.wait_ge(S.stored, 16)

@@ -2,14 +2,13 @@ from concourse.bass import DstId, RemoteDMATransfer
 from concourse.mybir import AluOpType, AxisListType, ActivationFunctionType
 
 N, Q, D = 9, 32, 128
-NP = 4
 G = 3
 P = G * Q
+NE = 2
 
 SCRATCH = {
-    "land_o": ("dram", [N, NP * 128, 8], "bfloat16"),
-    "land_ml": ("dram", [N, 128, 4], "float32"),
-    "zero": ("sbuf", [128, 2 * Q], "float32"),
+    "land_o": ("dram", [N, 128, 32], "bfloat16"),
+    "land_ml": ("dram", [N, 128, 1], "float32"),
     "mT": ("sbuf", [128, 2 * Q], "float32"),
     "o_sb": ("sbuf", [128, G, D], "bfloat16"),
     "V": ("sbuf", [128, Q], "float32"),
@@ -27,8 +26,8 @@ SCRATCH = {
     "Po0": ("psum", [128, 512], "float32"),
     "Po1": ("psum", [128, 512], "float32"),
 }
-SEMAPHORES = ["zs", "ld_ml", "ld_o", "sent", "ml_arr", "o_arr", "ml_in", "o_in", "iota", "cst", "pm", "pl", "nm", "xs",
-              "la", "act", "w0", "w1", "w2", "pd", "po0", "po1", "rs", "yd", "stored"]
+SEMAPHORES = ["ld_ml", "ld_o", "sent", "ml_arr", "o_arr", "ml_in", "o_in0", "o_in1", "o_in2", "iota", "cst", "pm", "pl",
+              "nm", "xs", "la", "act", "w0", "w1", "w2", "pd", "po0", "po1", "rs", "yd", "stored"]
 
 
 def rank_program(g, core, T, topo):
@@ -40,19 +39,9 @@ def rank_program(g, core, T, topo):
     Sq, Cp = ActivationFunctionType.Square, ActivationFunctionType.Copy
     A = AluOpType
 
-    ve.memset(T.zero[0:7, :], 0.0).then_inc(S.zs, 1)
-    sy.dma_start(T.land_ml[rank, 0:16, :], T.ml[:]).then_inc(S.ld_ml, 16)
+    sy.dma_start(T.land_ml[rank, 0:64, :], T.ml[:]).then_inc(S.ld_ml, 16)
     ac.dma_start(T.land_o[rank], T.o[:]).then_inc(S.ld_o, 16)
-    sy.wait_ge(S.zs, 1)
-    sy.dma_start(T.land_ml[rank, 16:128, :], T.zero[0:7, :]).then_inc(S.ld_ml, 16)
-
-    g.iota(T.V[0:P, :], [[-1, Q]], 0, 1, allow_small_or_imprecise_dtypes=True).then_inc(S.iota, 1)
-    ve.wait_ge(S.iota, 1)
-    ve.tensor_scalar(T.E[0:N, 0:N], T.V[0:N, 0:N], 0.0, None, A.is_equal).then_inc(S.cst, 1)
-    ve.tensor_scalar(T.E[0:N, N:15], T.V[0:N, N:15], float(-N), None, A.is_equal).then_inc(S.cst, 1)
-    for k in range(G):
-        ve.tensor_scalar(T.mask[Q * k:Q * k + Q, :], T.V[Q * k:Q * k + Q, :], float(Q * k), None,
-                         A.is_equal).then_inc(S.cst, 1)
+    sy.dma_start(T.land_ml[rank, 64:128, :], T.ml[:]).then_inc(S.ld_ml, 16)
 
     others = [T.cores[(rank + k) % N] for k in range(1, N)]
     usable = 0xFFFF
@@ -64,26 +53,35 @@ def rank_program(g, core, T, topo):
     for d in others:
         rid, pid = topo.addr(d, core)
         ids.append(DstId(rid=rid, pnc=pid))
-    ml_eng, o_eng = eng[0], [eng[2], eng[4], eng[6], eng[7]]
-    transfers = [RemoteDMATransfer(dst_ids=ids, dma_engine_mask=1 << ml_eng, remote_sem=S.ml_arr,
-                                   srcs=[T.land_ml[rank]], dsts=[T.land_ml[rank] for _ in others])]
-    for p in range(NP):
-        piece = T.land_o[rank, 128 * p:128 * p + 128, :]
-        transfers.append(RemoteDMATransfer(dst_ids=ids, dma_engine_mask=1 << o_eng[p], remote_sem=S.o_arr,
-                                           srcs=[piece], dsts=[piece for _ in others]))
     g.wait_ge(S.ld_ml, 32)
+    g.remote_dma_fused([RemoteDMATransfer(dst_ids=ids, dma_engine_mask=1 << eng[0], remote_sem=S.ml_arr,
+                                          srcs=[T.land_ml[rank]], dsts=[T.land_ml[rank] for _ in others])],
+                       local_sem=S.sent)
+    o_eng = eng[0::2][:NE]
+    ne = len(o_eng)
+    transfers = [RemoteDMATransfer(dst_ids=ids[k::ne], dma_engine_mask=1 << o_eng[k], remote_sem=S.o_arr,
+                                   srcs=[T.land_o[rank]], dsts=[T.land_o[rank] for _ in ids[k::ne]])
+                 for k in range(ne)]
     g.wait_ge(S.ld_o, 16)
     g.remote_dma_fused(transfers, local_sem=S.sent)
-    g.wait_ge(S.sent, 1 + NP)
+
+    g.iota(T.V[0:P, :], [[-1, Q]], 0, 1, allow_small_or_imprecise_dtypes=True).then_inc(S.iota, 1)
+    g.wait_ge(S.sent, 1 + ne)
+    ve.wait_ge(S.iota, 1)
+    ve.tensor_scalar(T.E[0:N, 0:N], T.V[0:N, 0:N], 0.0, None, A.is_equal).then_inc(S.cst, 1)
+    ve.tensor_scalar(T.E[0:N, N:15], T.V[0:N, N:15], float(-N), None, A.is_equal).then_inc(S.cst, 1)
+    for k in range(G):
+        ve.tensor_scalar(T.mask[Q * k:Q * k + Q, :], T.V[Q * k:Q * k + Q, :], float(Q * k), None,
+                         A.is_equal).then_inc(S.cst, 1)
 
     sy.wait_ge(S.ld_ml, 32)
     sy.wait_ge(S.ml_arr, N - 1)
-    sy.dma_start(T.mT[0:N, :], T.land_ml[:, 0:16, :]).then_inc(S.ml_in, 16)
+    sy.dma_start(T.mT[0:N, :], T.land_ml[:, 0:64, :]).then_inc(S.ml_in, 16)
     for q_, cs in ((sy, (0,)), (ac, (1, 2))):
         q_.wait_ge(S.ld_o, 16)
-        q_.wait_ge(S.o_arr, (N - 1) * NP)
+        q_.wait_ge(S.o_arr, N - 1)
         for c in cs:
-            q_.dma_start(T.o_sb[0:P, c, :], T.land_o[c::G]).then_inc(S.o_in, 16)
+            q_.dma_start(T.o_sb[0:P, c, :], T.land_o[c::G]).then_inc(S["o_in%d" % c], 16)
 
     te.wait_ge(S.cst, 5)
     te.wait_ge(S.ml_in, 16)
@@ -122,16 +120,17 @@ def rank_program(g, core, T, topo):
     for c in range(G):
         te.wait_ge(S["w%d" % c], 1)
         te.matmul(T.Pd[0:Q, 0:1], T.W[0:P, c, :], T.lA[0:P, c:c + 1], c == 0, c == G - 1).then_inc(S.pd, 1)
-    te.wait_ge(S.o_in, 16 * G)
     H = D // 2
-    for h, (Po, sem) in enumerate(((T.Po0, S.po0), (T.Po1, S.po1))):
-        for c in range(G):
+    halves = ((T.Po0, S.po0), (T.Po1, S.po1))
+    for c in range(G):
+        te.wait_ge(S["o_in%d" % c], 16)
+        for h, (Po, sem) in enumerate(halves):
             te.matmul(Po[0:Q, 0:H], T.W[0:P, c, :], T.o_sb[0:P, c, H * h:H * h + H], c == 0, c == G - 1).then_inc(sem, 1)
 
     ve.wait_ge(S.pd, G)
     ve.reciprocal(T.r[0:Q, :], T.Pd[0:Q, 0:1]).then_inc(S.rs, 1)
     ve.wait_ge(S.rs, 1)
-    for h, (Po, sem) in enumerate(((T.Po0, S.po0), (T.Po1, S.po1))):
+    for h, (Po, sem) in enumerate(halves):
         ve.wait_ge(sem, G)
         ve.tensor_scalar(T.y_sb[0:Q, H * h:H * h + H], Po[0:Q, 0:H], T.r[0:Q, 0:1], None, A.mult).then_inc(S.yd, 1)
     sy.wait_ge(S.yd, 2)

@@ -2,32 +2,53 @@ from concourse.bass import DstId, RemoteDMATransfer
 from concourse.mybir import AluOpType, AxisListType, ActivationFunctionType
 
 N, Q, D = 9, 32, 128
-G = 3
-P = G * Q
+K = N - 1
+NA = 16
+NB = 2
 NE = 2
+H = D // 2
+MAGIC = 12582912.0
 
 SCRATCH = {
-    "land_o": ("dram", [N, 128, 32], "bfloat16"),
-    "land_ml": ("dram", [N, 128, 1], "float32"),
-    "mT": ("sbuf", [128, 2 * Q], "float32"),
-    "o_sb": ("sbuf", [128, G, D], "bfloat16"),
-    "V": ("sbuf", [128, Q], "float32"),
-    "mask": ("sbuf", [128, Q], "bfloat16"),
-    "E": ("sbuf", [128, 16], "float32"),
-    "negM": ("sbuf", [128, 1], "float32"),
-    "ch": ("sbuf", [128, 24], "float32"),
-    "lA": ("sbuf", [128, 4], "bfloat16"),
-    "W": ("sbuf", [128, G, Q], "bfloat16"),
-    "r": ("sbuf", [128, 1], "float32"),
-    "y_sb": ("sbuf", [128, D], "bfloat16"),
+    "src_o": ("dram", [128, 32], "bfloat16"),
+    "src_ml": ("dram", [128, 1], "float32"),
+    "land_o": ("dram", [K, 128, 32], "bfloat16"),
+    "land_ml": ("dram", [K, 128, 1], "float32"),
+    "mk": ("sbuf", [128, 4], "float32"),
+    "mown": ("sbuf", [128, 4], "float32"),
+    "o_sb": ("sbuf", [128, NB * D], "bfloat16"),
+    "o_own": ("sbuf", [128, NB * D], "bfloat16"),
+    "v2": ("sbuf", [128, NA], "float32"),
+    "u2": ("sbuf", [128, NA], "float32"),
+    "t1": ("sbuf", [128, NA], "float32"),
+    "t2": ("sbuf", [128, NA], "float32"),
+    "t3": ("sbuf", [128, NA], "float32"),
+    "negmask": ("sbuf", [128, NA], "float32"),
+    "T16b": ("sbuf", [128, NA], "bfloat16"),
+    "R": ("sbuf", [128, 128], "bfloat16"),
+    "cl": ("sbuf", [128, NA], "float32"),
+    "maskJ": ("sbuf", [128, NA], "float32"),
+    "Dm": ("sbuf", [128, NB * NA], "bfloat16"),
+    "Down": ("sbuf", [128, NB * NA], "bfloat16"),
+    "nm": ("sbuf", [128, NB, NA], "float32"),
+    "nmo": ("sbuf", [128, NB, NA], "float32"),
+    "negM": ("sbuf", [128, 4], "float32"),
+    "lk": ("sbuf", [128, 8], "bfloat16"),
+    "lo": ("sbuf", [128, 8], "bfloat16"),
+    "W": ("sbuf", [128, NB, NA], "bfloat16"),
+    "Wo": ("sbuf", [128, NB, NA], "bfloat16"),
+    "r": ("sbuf", [128, 4], "float32"),
+    "y_sb": ("sbuf", [128, NB * D], "bfloat16"),
     "Pm": ("psum", [128, 512], "float32"),
-    "Pl": ("psum", [128, 512], "float32"),
     "Pd": ("psum", [128, 512], "float32"),
     "Po0": ("psum", [128, 512], "float32"),
     "Po1": ("psum", [128, 512], "float32"),
+    "Po2": ("psum", [128, 512], "float32"),
+    "Po3": ("psum", [128, 512], "float32"),
 }
-SEMAPHORES = ["ld_ml", "ld_o", "sent", "ml_arr", "o_arr", "ml_in", "o_in0", "o_in1", "o_in2", "iota", "cst", "pm", "pl",
-              "nm", "xs", "la", "act", "w0", "w1", "w2", "pd", "po0", "po1", "rs", "yd", "stored"]
+SEMAPHORES = ["ld_ml", "ld_o", "ld_mo", "ld_oo", "sent", "ml_arr", "o_arr", "ml_in", "o_in", "io1", "io2", "c1", "c2",
+              "c3", "c4", "c5", "c6", "dm", "la", "pm", "n0", "n1", "nmk", "wo0", "wo1", "w0", "w1", "pd", "po0", "po1",
+              "po2", "po3", "rs", "yd", "stored"]
 
 
 def rank_program(g, core, T, topo):
@@ -36,14 +57,20 @@ def rank_program(g, core, T, topo):
         return
     S = T.sem
     sy, ac, ve, te = g.sync, g.scalar, g.vector, g.tensor
-    Sq, Cp = ActivationFunctionType.Square, ActivationFunctionType.Copy
+    Exp, Cp, Idn = ActivationFunctionType.Exp, ActivationFunctionType.Copy, ActivationFunctionType.Identity
     A = AluOpType
 
-    sy.dma_start(T.land_ml[rank, 0:64, :], T.ml[:]).then_inc(S.ld_ml, 16)
-    ac.dma_start(T.land_o[rank], T.o[:]).then_inc(S.ld_o, 16)
-    sy.dma_start(T.land_ml[rank, 64:128, :], T.ml[:]).then_inc(S.ld_ml, 16)
+    sy.dma_start(T.src_ml[0:2 * Q, :], T.ml[:]).then_inc(S.ld_ml, 16)
+    ac.dma_start(T.src_ml[2 * Q:4 * Q, :], T.ml[:]).then_inc(S.ld_ml, 16)
+    ac.dma_start(T.src_o[:], T.o[:]).then_inc(S.ld_o, 16)
+    sy.dma_start(T.mown[0:NA, :], T.ml[:]).then_inc(S.ld_mo, 16)
+    ac.dma_start(T.o_own[0:NA, :], T.o[:]).then_inc(S.ld_oo, 16)
 
-    others = [T.cores[(rank + k) % N] for k in range(1, N)]
+    g.iota(T.v2[:, :], [[-1, NA]], 0, 1, allow_small_or_imprecise_dtypes=True).then_inc(S.io1, 1)
+
+    steps = list(range(1, N))
+    others = [T.cores[(rank + t) % N] for t in steps]
+    slots = [K - t for t in steps]
     usable = 0xFFFF
     for d in others:
         assert topo.may_write(core, d)
@@ -55,84 +82,117 @@ def rank_program(g, core, T, topo):
         ids.append(DstId(rid=rid, pnc=pid))
     g.wait_ge(S.ld_ml, 32)
     g.remote_dma_fused([RemoteDMATransfer(dst_ids=ids, dma_engine_mask=1 << eng[0], remote_sem=S.ml_arr,
-                                          srcs=[T.land_ml[rank]], dsts=[T.land_ml[rank] for _ in others])],
+                                          srcs=[T.src_ml[:]], dsts=[T.land_ml[k] for k in slots])],
                        local_sem=S.sent)
     o_eng = eng[0::2][:NE]
     ne = len(o_eng)
-    transfers = [RemoteDMATransfer(dst_ids=ids[k::ne], dma_engine_mask=1 << o_eng[k], remote_sem=S.o_arr,
-                                   srcs=[T.land_o[rank]], dsts=[T.land_o[rank] for _ in ids[k::ne]])
-                 for k in range(ne)]
+    transfers = [RemoteDMATransfer(dst_ids=ids[i::ne], dma_engine_mask=1 << o_eng[i], remote_sem=S.o_arr,
+                                   srcs=[T.src_o[:]], dsts=[T.land_o[k] for k in slots[i::ne]])
+                 for i in range(ne)]
     g.wait_ge(S.ld_o, 16)
     g.remote_dma_fused(transfers, local_sem=S.sent)
-
-    g.iota(T.V[0:P, :], [[-1, Q]], 0, 1, allow_small_or_imprecise_dtypes=True).then_inc(S.iota, 1)
+    g.iota(T.u2[:, :], [[-NA, NA]], 0, 1, allow_small_or_imprecise_dtypes=True).then_inc(S.io2, 1)
     g.wait_ge(S.sent, 1 + ne)
-    ve.wait_ge(S.iota, 1)
-    ve.tensor_scalar(T.E[0:N, 0:N], T.V[0:N, 0:N], 0.0, None, A.is_equal).then_inc(S.cst, 1)
-    ve.tensor_scalar(T.E[0:N, N:15], T.V[0:N, N:15], float(-N), None, A.is_equal).then_inc(S.cst, 1)
-    for k in range(G):
-        ve.tensor_scalar(T.mask[Q * k:Q * k + Q, :], T.V[Q * k:Q * k + Q, :], float(Q * k), None,
-                         A.is_equal).then_inc(S.cst, 1)
 
-    sy.wait_ge(S.ld_ml, 32)
-    sy.wait_ge(S.ml_arr, N - 1)
-    sy.dma_start(T.mT[0:N, :], T.land_ml[:, 0:64, :]).then_inc(S.ml_in, 16)
-    for q_, cs in ((sy, (0,)), (ac, (1, 2))):
-        q_.wait_ge(S.ld_o, 16)
-        q_.wait_ge(S.o_arr, N - 1)
-        for c in cs:
-            q_.dma_start(T.o_sb[0:P, c, :], T.land_o[c::G]).then_inc(S["o_in%d" % c], 16)
+    ve.wait_ge(S.io1, 1)
+    ve.tensor_scalar(T.t1[:, :], T.v2[:, :], 1.0 / NA, MAGIC, A.mult, A.add).then_inc(S.c1, 1)
+    ve.wait_ge(S.c1, 1)
+    ve.tensor_scalar(T.t2[:, :], T.t1[:, :], MAGIC, float(NA), A.subtract, A.mult).then_inc(S.c1, 1)
+    ve.wait_ge(S.c1, 2)
+    ve.tensor_tensor(T.t3[:, :], T.t2[:, :], T.v2[:, :], A.not_equal).then_inc(S.c1, 1)
+    ve.wait_ge(S.c1, 3)
+    ve.tensor_scalar(T.negmask[:, :], T.t3[:, :], -30000.0, None, A.mult).then_inc(S.c1, 1)
+    ac.wait_ge(S.c1, 4)
+    ac.activation(T.T16b[:, :], T.negmask[:, :], Exp).then_inc(S.c2, 1)
+    ve.memset(T.Down[0:NA, :], 0.0).then_inc(S.c5, 1)
+    ve.wait_ge(S.c5, 1)
+    ve.wait_ge(S.ld_mo, 16)
+    ve.tensor_copy(T.Down[0:NA, K:NB * NA:NA], T.mown[0:NA, 0:4:2]).then_inc(S.c5, 1)
+    ve.tensor_copy(T.lo[0:NA, 0:NB], T.mown[0:NA, 1:4:2]).then_inc(S.c5, 1)
+    ve.wait_ge(S.c1, 4)
+    for b in range(NB):
+        ve.tensor_scalar(T.nmo[0:NA, b, :], T.negmask[0:NA, :], T.mown[0:NA, 2 * b:2 * b + 1], None,
+                         A.add).then_inc(S.c6, 1)
+    ve.wait_ge(S.c2, 1)
+    for k in range(K):
+        ve.tensor_copy(T.R[:, NA * k:NA * k + NA], T.T16b[:, :]).then_inc(S.c3, 1)
+    ve.wait_ge(S.io2, 1)
+    ve.tensor_scalar(T.cl[:, :], T.u2[:, :], 0.0, float(NA - 1), A.max, A.min).then_inc(S.c4, 1)
+    ve.wait_ge(S.c4, 1)
+    ve.tensor_tensor(T.maskJ[:, :], T.cl[:, :], T.u2[:, :], A.is_equal).then_inc(S.c4, 1)
+    ve.wait_ge(S.c4, 2)
 
-    te.wait_ge(S.cst, 5)
-    te.wait_ge(S.ml_in, 16)
-    for k in range(G):
-        te.matmul(T.Pm[Q * k:Q * k + Q, 0:N], T.mT[0:N, 0:2 * Q:2], T.E[0:N, G * k:G * k + N], True, True).then_inc(S.pm, 1)
-    for k in range(G):
-        te.matmul(T.Pl[Q * k:Q * k + Q, 0:G], T.mT[0:N, 1:2 * Q:2], T.E[0:N, G * k:G * k + G], True, True).then_inc(S.pl, 1)
+    sy.wait_ge(S.ml_arr, K)
+    sy.dma_start(T.mk[:, :], T.land_ml[:, 0:2 * Q, :]).then_inc(S.ml_in, 16)
+    sy.wait_ge(S.o_arr, K)
+    sy.dma_start(T.o_sb[:, :], T.land_o[:]).then_inc(S.o_in, 16)
 
-    ve.wait_ge(S.pm, G)
-    ve.tensor_reduce(T.negM[0:P, :], T.Pm[0:P, 0:N], AxisListType.X, A.max, negate=True).then_inc(S.nm, 1)
-    ve.wait_ge(S.nm, 1)
-    ve.tensor_scalar(T.ch[0:P, 0:G], T.Pm[0:P, 0:G], T.negM[0:P, 0:1], -16.0, A.add, A.max).then_inc(S.xs, 1)
-    ve.wait_ge(S.pl, G)
-    ve.tensor_copy(T.lA[0:P, 0:G], T.Pl[0:P, 0:G]).then_inc(S.la, 1)
+    te.wait_ge(S.c3, K)
+    te.wait_ge(S.c5, 3)
+    te.matmul(T.Pm[:, 0:NB * NA], T.R[0:NA, :], T.Down[0:NA, :], True, False)
+    ve.wait_ge(S.ml_in, 16)
+    ve.tensor_scalar(T.Dm[:, 0:NA], T.maskJ[:, :], T.mk[:, 0:1], None, A.mult).then_inc(S.dm, 1)
+    ve.tensor_copy(T.lk[:, 0:NB], T.mk[:, 1:4:2]).then_inc(S.la, 1)
+    ac.wait_ge(S.c4, 2)
+    ac.wait_ge(S.ml_in, 16)
+    ac.activation(T.Dm[:, NA:2 * NA], T.maskJ[:, :], Cp, scale=T.mk[:, 2:3]).then_inc(S.dm, 1)
+    for b in range(NB):
+        ac.activation(T.nm[:, b, :], T.negmask[:, :], Idn, bias=T.mk[:, 2 * b:2 * b + 1]).then_inc(S.nmk, 1)
+    te.wait_ge(S.dm, NB)
+    te.matmul(T.Pm[:, 0:NB * NA], T.R[:, :], T.Dm[:, :], False, True).then_inc(S.pm, 1)
+    ve.wait_ge(S.pm, 1)
+    nsem = (S.n0, S.n1)
+    for b in range(NB):
+        ve.tensor_reduce(T.negM[:, b:b + 1], T.Pm[:, NA * b:NA * b + N], AxisListType.X, A.max,
+                         negate=True).then_inc(nsem[b], 1)
 
-    def col(i):
-        return T.ch[0:P, 4 * i:4 * i + G]
-    ac.wait_ge(S.xs, 1)
-    ac.activation(col(1), col(0), Sq, bias=1.0, scale=1.0 / 16.0).then_inc(S.act, 1)
-    ac.wait_ge(S.act, 1)
-    ac.activation(col(2), col(1), Sq, bias=1.0).then_inc(S.act, 1)
-    for i in (2, 3, 4):
-        ac.wait_ge(S.act, i)
-        ac.activation(col(i + 1), col(i), Sq).then_inc(S.act, 1)
-    f0 = 20
+    wo, w = (S.wo0, S.wo1), (S.w0, S.w1)
+    ac.wait_ge(S.nmk, NB)
+    ac.wait_ge(S.c6, NB)
+    for b in range(NB):
+        ac.wait_ge(nsem[b], 1)
+        ac.activation(T.Wo[0:NA, b, :], T.nmo[0:NA, b, :], Exp, bias=T.negM[0:NA, b:b + 1]).then_inc(wo[b], 1)
+    for b in range(NB):
+        ac.activation(T.W[:, b, :], T.nm[:, b, :], Exp, bias=T.negM[:, b:b + 1]).then_inc(w[b], 1)
 
-    ac.wait_ge(S.act, 5)
-    ac.wait_ge(S.cst, 5)
-    ac.activation(T.W[0:P, 1, :], T.mask[0:P, :], Cp, scale=T.ch[0:P, f0 + 1:f0 + 2]).then_inc(S.w1, 1)
-    ve.wait_ge(S.act, 5)
-    ve.wait_ge(S.cst, 5)
-    ve.tensor_scalar(T.W[0:P, 0, :], T.mask[0:P, :], T.ch[0:P, f0:f0 + 1], None, A.mult).then_inc(S.w0, 1)
-    ve.tensor_scalar(T.W[0:P, 2, :], T.mask[0:P, :], T.ch[0:P, f0 + 2:f0 + 3], None, A.mult).then_inc(S.w2, 1)
+    Po = (T.Po0, T.Po1, T.Po2, T.Po3)
+    po = (S.po0, S.po1, S.po2, S.po3)
 
+    def own(i):
+        te.matmul(Po[i][0:NA, 0:H], T.Wo[0:NA, i // 2, :], T.o_own[0:NA, H * i:H * i + H], True, False)
+
+    def den(b):
+        te.wait_ge(w[b], 1)
+        te.matmul(T.Pd[0:NA, b:b + 1], T.Wo[0:NA, b, :], T.lo[0:NA, b:b + 1], True, False)
+        te.matmul(T.Pd[0:NA, b:b + 1], T.W[:, b, :], T.lk[:, b:b + 1], False, True).then_inc(S.pd, 1)
+
+    te.wait_ge(S.ld_oo, 16)
     te.wait_ge(S.la, 1)
-    for c in range(G):
-        te.wait_ge(S["w%d" % c], 1)
-        te.matmul(T.Pd[0:Q, 0:1], T.W[0:P, c, :], T.lA[0:P, c:c + 1], c == 0, c == G - 1).then_inc(S.pd, 1)
-    H = D // 2
-    halves = ((T.Po0, S.po0), (T.Po1, S.po1))
-    for c in range(G):
-        te.wait_ge(S["o_in%d" % c], 16)
-        for h, (Po, sem) in enumerate(halves):
-            te.matmul(Po[0:Q, 0:H], T.W[0:P, c, :], T.o_sb[0:P, c, H * h:H * h + H], c == 0, c == G - 1).then_inc(sem, 1)
+    te.wait_ge(wo[0], 1)
+    own(0)
+    own(1)
+    den(0)
+    te.wait_ge(wo[1], 1)
+    own(2)
+    den(1)
+    own(3)
+    te.wait_ge(S.o_in, 16)
+    for i in range(4):
+        te.matmul(Po[i][0:NA, 0:H], T.W[:, i // 2, :], T.o_sb[:, H * i:H * i + H], False, True).then_inc(po[i], 1)
 
-    ve.wait_ge(S.pd, G)
-    ve.reciprocal(T.r[0:Q, :], T.Pd[0:Q, 0:1]).then_inc(S.rs, 1)
+    ve.wait_ge(S.pd, NB)
+    ve.reciprocal(T.r[0:NA, 0:NB], T.Pd[0:NA, 0:NB]).then_inc(S.rs, 1)
     ve.wait_ge(S.rs, 1)
-    for h, (Po, sem) in enumerate(halves):
-        ve.wait_ge(sem, G)
-        ve.tensor_scalar(T.y_sb[0:Q, H * h:H * h + H], Po[0:Q, 0:H], T.r[0:Q, 0:1], None, A.mult).then_inc(S.yd, 1)
-    sy.wait_ge(S.yd, 2)
-    sy.dma_start(T.y[:], T.y_sb[0:Q, :]).then_inc(S.stored, 16)
+    ac.wait_ge(S.rs, 1)
+    for i in range(4):
+        b = i // 2
+        if i % 2 == 0:
+            ac.wait_ge(po[i], 1)
+            ac.activation(T.y_sb[0:NA, H * i:H * i + H], Po[i][0:NA, 0:H], Cp, scale=T.r[0:NA, b:b + 1]).then_inc(S.yd, 1)
+        else:
+            ve.wait_ge(po[i], 1)
+            ve.tensor_scalar(T.y_sb[0:NA, H * i:H * i + H], Po[i][0:NA, 0:H], T.r[0:NA, b:b + 1], None,
+                             A.mult).then_inc(S.yd, 1)
+    sy.wait_ge(S.yd, 4)
+    sy.dma_start(T.y[:], T.y_sb[0:NA, :]).then_inc(S.stored, 16)
     sy.wait_ge(S.stored, 16)

from concourse.bass import DstId, RemoteDMATransfer
from concourse.mybir import AluOpType, AxisListType, ActivationFunctionType

N, Q, D = 9, 32, 128
K = N - 1
NA = 16
NB = 2
NE = 2
H = D // 2
MAGIC = 12582912.0

SCRATCH = {
    "src_o": ("dram", [128, 32], "bfloat16"),
    "src_ml": ("dram", [128, 1], "float32"),
    "land_o": ("dram", [K, 128, 32], "bfloat16"),
    "land_ml": ("dram", [K, 128, 1], "float32"),
    "mk": ("sbuf", [128, 4], "float32"),
    "mown": ("sbuf", [128, 4], "float32"),
    "o_sb": ("sbuf", [128, NB * D], "bfloat16"),
    "o_own": ("sbuf", [128, NB * D], "bfloat16"),
    "v2": ("sbuf", [128, NA], "float32"),
    "u2": ("sbuf", [128, NA], "float32"),
    "t1": ("sbuf", [128, NA], "float32"),
    "t2": ("sbuf", [128, NA], "float32"),
    "t3": ("sbuf", [128, NA], "float32"),
    "negmask": ("sbuf", [128, NA], "float32"),
    "T16b": ("sbuf", [128, NA], "bfloat16"),
    "R": ("sbuf", [128, 128], "bfloat16"),
    "cl": ("sbuf", [128, NA], "float32"),
    "maskJ": ("sbuf", [128, NA], "float32"),
    "Dm": ("sbuf", [128, NB * NA], "bfloat16"),
    "Down": ("sbuf", [128, NB * NA], "bfloat16"),
    "nm": ("sbuf", [128, NB, NA], "float32"),
    "nmo": ("sbuf", [128, NB, NA], "float32"),
    "negM": ("sbuf", [128, 4], "float32"),
    "lk": ("sbuf", [128, 8], "bfloat16"),
    "lo": ("sbuf", [128, 8], "bfloat16"),
    "W": ("sbuf", [128, NB, NA], "bfloat16"),
    "Wo": ("sbuf", [128, NB, NA], "bfloat16"),
    "r": ("sbuf", [128, 4], "float32"),
    "y_sb": ("sbuf", [128, NB * D], "bfloat16"),
    "Pm": ("psum", [128, 512], "float32"),
    "Pd": ("psum", [128, 512], "float32"),
    "Po0": ("psum", [128, 512], "float32"),
    "Po1": ("psum", [128, 512], "float32"),
    "Po2": ("psum", [128, 512], "float32"),
    "Po3": ("psum", [128, 512], "float32"),
}
SEMAPHORES = ["ld_ml", "ld_o", "ld_mo", "ld_oo", "sent", "ml_arr", "o_arr", "ml_in", "o_in", "io1", "io2", "c1", "c2",
              "c3", "c4", "c5", "c6", "dm", "la", "pm", "n0", "n1", "nmk", "wo0", "wo1", "w0", "w1", "pd", "po0", "po1",
              "po2", "po3", "rs", "yd", "stored"]


def rank_program(g, core, T, topo):
    rank = T.rank_of(core)
    if rank is None:
        return
    S = T.sem
    sy, ac, ve, te = g.sync, g.scalar, g.vector, g.tensor
    Exp, Cp, Idn = ActivationFunctionType.Exp, ActivationFunctionType.Copy, ActivationFunctionType.Identity
    A = AluOpType

    sy.dma_start(T.src_ml[0:2 * Q, :], T.ml[:]).then_inc(S.ld_ml, 16)
    ac.dma_start(T.src_ml[2 * Q:4 * Q, :], T.ml[:]).then_inc(S.ld_ml, 16)
    ac.dma_start(T.src_o[:], T.o[:]).then_inc(S.ld_o, 16)
    sy.dma_start(T.mown[0:NA, :], T.ml[:]).then_inc(S.ld_mo, 16)
    ac.dma_start(T.o_own[0:NA, :], T.o[:]).then_inc(S.ld_oo, 16)

    g.iota(T.v2[:, :], [[-1, NA]], 0, 1, allow_small_or_imprecise_dtypes=True).then_inc(S.io1, 1)

    steps = list(range(1, N))
    others = [T.cores[(rank + t) % N] for t in steps]
    slots = [K - t for t in steps]
    usable = 0xFFFF
    for d in others:
        assert topo.may_write(core, d)
        usable &= topo.mask(core, d)
    eng = [e for e in range(16) if (usable >> e) & 1]
    ids = []
    for d in others:
        rid, pid = topo.addr(d, core)
        ids.append(DstId(rid=rid, pnc=pid))
    g.wait_ge(S.ld_ml, 32)
    g.remote_dma_fused([RemoteDMATransfer(dst_ids=ids, dma_engine_mask=1 << eng[0], remote_sem=S.ml_arr,
                                          srcs=[T.src_ml[:]], dsts=[T.land_ml[k] for k in slots])],
                       local_sem=S.sent)
    o_eng = eng[0::2][:NE]
    ne = len(o_eng)
    transfers = [RemoteDMATransfer(dst_ids=ids[i::ne], dma_engine_mask=1 << o_eng[i], remote_sem=S.o_arr,
                                   srcs=[T.src_o[:]], dsts=[T.land_o[k] for k in slots[i::ne]])
                 for i in range(ne)]
    g.wait_ge(S.ld_o, 16)
    g.remote_dma_fused(transfers, local_sem=S.sent)
    g.iota(T.u2[:, :], [[-NA, NA]], 0, 1, allow_small_or_imprecise_dtypes=True).then_inc(S.io2, 1)
    g.wait_ge(S.sent, 1 + ne)

    ve.wait_ge(S.io1, 1)
    ve.tensor_scalar(T.t1[:, :], T.v2[:, :], 1.0 / NA, MAGIC, A.mult, A.add).then_inc(S.c1, 1)
    ve.wait_ge(S.c1, 1)
    ve.tensor_scalar(T.t2[:, :], T.t1[:, :], MAGIC, float(NA), A.subtract, A.mult).then_inc(S.c1, 1)
    ve.wait_ge(S.c1, 2)
    ve.tensor_tensor(T.t3[:, :], T.t2[:, :], T.v2[:, :], A.not_equal).then_inc(S.c1, 1)
    ve.wait_ge(S.c1, 3)
    ve.tensor_scalar(T.negmask[:, :], T.t3[:, :], -30000.0, None, A.mult).then_inc(S.c1, 1)
    ac.wait_ge(S.c1, 4)
    ac.activation(T.T16b[:, :], T.negmask[:, :], Exp).then_inc(S.c2, 1)
    ve.memset(T.Down[0:NA, :], 0.0).then_inc(S.c5, 1)
    ve.wait_ge(S.c5, 1)
    ve.wait_ge(S.ld_mo, 16)
    ve.tensor_copy(T.Down[0:NA, K:NB * NA:NA], T.mown[0:NA, 0:4:2]).then_inc(S.c5, 1)
    ve.tensor_copy(T.lo[0:NA, 0:NB], T.mown[0:NA, 1:4:2]).then_inc(S.c5, 1)
    ve.wait_ge(S.c1, 4)
    for b in range(NB):
        ve.tensor_scalar(T.nmo[0:NA, b, :], T.negmask[0:NA, :], T.mown[0:NA, 2 * b:2 * b + 1], None,
                         A.add).then_inc(S.c6, 1)
    ve.wait_ge(S.c2, 1)
    for k in range(K):
        ve.tensor_copy(T.R[:, NA * k:NA * k + NA], T.T16b[:, :]).then_inc(S.c3, 1)
    ve.wait_ge(S.io2, 1)
    ve.tensor_scalar(T.cl[:, :], T.u2[:, :], 0.0, float(NA - 1), A.max, A.min).then_inc(S.c4, 1)
    ve.wait_ge(S.c4, 1)
    ve.tensor_tensor(T.maskJ[:, :], T.cl[:, :], T.u2[:, :], A.is_equal).then_inc(S.c4, 1)
    ve.wait_ge(S.c4, 2)

    sy.wait_ge(S.ml_arr, K)
    sy.dma_start(T.mk[:, :], T.land_ml[:, 0:2 * Q, :]).then_inc(S.ml_in, 16)
    sy.wait_ge(S.o_arr, K)
    sy.dma_start(T.o_sb[:, :], T.land_o[:]).then_inc(S.o_in, 16)

    te.wait_ge(S.c3, K)
    te.wait_ge(S.c5, 3)
    te.matmul(T.Pm[:, 0:NB * NA], T.R[0:NA, :], T.Down[0:NA, :], True, False)
    ve.wait_ge(S.ml_in, 16)
    ve.tensor_scalar(T.Dm[:, 0:NA], T.maskJ[:, :], T.mk[:, 0:1], None, A.mult).then_inc(S.dm, 1)
    ve.tensor_copy(T.lk[:, 0:NB], T.mk[:, 1:4:2]).then_inc(S.la, 1)
    ac.wait_ge(S.c4, 2)
    ac.wait_ge(S.ml_in, 16)
    ac.activation(T.Dm[:, NA:2 * NA], T.maskJ[:, :], Cp, scale=T.mk[:, 2:3]).then_inc(S.dm, 1)
    for b in range(NB):
        ac.activation(T.nm[:, b, :], T.negmask[:, :], Idn, bias=T.mk[:, 2 * b:2 * b + 1]).then_inc(S.nmk, 1)
    te.wait_ge(S.dm, NB)
    te.matmul(T.Pm[:, 0:NB * NA], T.R[:, :], T.Dm[:, :], False, True).then_inc(S.pm, 1)
    ve.wait_ge(S.pm, 1)
    nsem = (S.n0, S.n1)
    for b in range(NB):
        ve.tensor_reduce(T.negM[:, b:b + 1], T.Pm[:, NA * b:NA * b + N], AxisListType.X, A.max,
                         negate=True).then_inc(nsem[b], 1)

    wo, w = (S.wo0, S.wo1), (S.w0, S.w1)
    ac.wait_ge(S.nmk, NB)
    ac.wait_ge(S.c6, NB)
    for b in range(NB):
        ac.wait_ge(nsem[b], 1)
        ac.activation(T.Wo[0:NA, b, :], T.nmo[0:NA, b, :], Exp, bias=T.negM[0:NA, b:b + 1]).then_inc(wo[b], 1)
    for b in range(NB):
        ac.activation(T.W[:, b, :], T.nm[:, b, :], Exp, bias=T.negM[:, b:b + 1]).then_inc(w[b], 1)

    Po = (T.Po0, T.Po1, T.Po2, T.Po3)
    po = (S.po0, S.po1, S.po2, S.po3)

    def own(i):
        te.matmul(Po[i][0:NA, 0:H], T.Wo[0:NA, i // 2, :], T.o_own[0:NA, H * i:H * i + H], True, False)

    def den(b):
        te.wait_ge(w[b], 1)
        te.matmul(T.Pd[0:NA, b:b + 1], T.Wo[0:NA, b, :], T.lo[0:NA, b:b + 1], True, False)
        te.matmul(T.Pd[0:NA, b:b + 1], T.W[:, b, :], T.lk[:, b:b + 1], False, True).then_inc(S.pd, 1)

    te.wait_ge(S.ld_oo, 16)
    te.wait_ge(S.la, 1)
    te.wait_ge(wo[0], 1)
    own(0)
    own(1)
    den(0)
    te.wait_ge(wo[1], 1)
    own(2)
    den(1)
    own(3)
    te.wait_ge(S.o_in, 16)
    for i in range(4):
        te.matmul(Po[i][0:NA, 0:H], T.W[:, i // 2, :], T.o_sb[:, H * i:H * i + H], False, True).then_inc(po[i], 1)

    ve.wait_ge(S.pd, NB)
    ve.reciprocal(T.r[0:NA, 0:NB], T.Pd[0:NA, 0:NB]).then_inc(S.rs, 1)
    ve.wait_ge(S.rs, 1)
    ac.wait_ge(S.rs, 1)
    for i in range(4):
        b = i // 2
        if i % 2 == 0:
            ac.wait_ge(po[i], 1)
            ac.activation(T.y_sb[0:NA, H * i:H * i + H], Po[i][0:NA, 0:H], Cp, scale=T.r[0:NA, b:b + 1]).then_inc(S.yd, 1)
        else:
            ve.wait_ge(po[i], 1)
            ve.tensor_scalar(T.y_sb[0:NA, H * i:H * i + H], Po[i][0:NA, 0:H], T.r[0:NA, b:b + 1], None,
                             A.mult).then_inc(S.yd, 1)
    sy.wait_ge(S.yd, 4)
    sy.dma_start(T.y[:], T.y_sb[0:NA, :]).then_inc(S.stored, 16)
    sy.wait_ge(S.stored, 16)
